import numpy as np
import ml_dtypes


def mxq(x, axis, fmt="e4m3"):
    dtype, down = {"e4m3": (ml_dtypes.float8_e4m3fn, 7), "e5m2": (ml_dtypes.float8_e5m2, 14)}[fmt]
    v = np.moveaxis(np.asarray(x, np.float32).astype(ml_dtypes.bfloat16).astype(np.float64), axis, -1)
    blocks = v.reshape(v.shape[:-1] + (-1, 32))
    amax = np.abs(blocks).max(-1, keepdims=True)
    byte = np.maximum(np.where(amax > 0, np.frexp(amax)[1] - 1 + 127, 0) - down, 1)
    scale = np.exp2(byte - 127.0)
    codes = (blocks / scale).astype(np.float32).astype(dtype).astype(np.float64)
    return np.moveaxis((codes * scale).reshape(v.shape), -1, axis)


WIDE = False


def mx_kscale(k):
    if not WIDE:
        return np.ones(k)
    levels = np.array([10, -10, 5, -5, 0])
    if k % 512:
        return np.exp2(np.random.permutation(np.resize(levels, k // 32))).repeat(32)
    a = np.empty((k // 512, 16))
    for p in range(k // 512):
        a[p, :8] = np.random.permutation(np.resize(levels, 8))
        for g in range(8):
            far = levels[np.abs(levels - a[p, g]) >= 10]
            a[p, g + 8] = far[np.random.randint(len(far))]
    return np.exp2(a.ravel()).repeat(32)


def f64(x):
    return np.asarray(x).astype(np.float64)


def striped(idx):
    return np.tile(idx.reshape(-1, 16).T, (8, 1)).astype(np.uint16)


def unstriped(offs):
    return offs[:16].T.reshape(-1).astype(np.int64)


E2M1 = np.array([0.0, 0.5, 1.0, 1.5, 2.0, 3.0, 4.0, 6.0, -0.0, -0.5, -1.0, -1.5, -2.0, -3.0, -4.0, -6.0])


def pack_weight(w, fmt):
    k, n = w.shape
    w = f64(np.asarray(w, np.float32).astype(ml_dtypes.bfloat16)).reshape(k // 32, 32, n)
    amax = np.abs(w).max(1)
    if fmt == "e4m3":
        byte = np.frexp(amax)[1] - 1 + 127 - 7
    else:
        mant, ex = np.frexp(amax / 6.0)
        byte = np.where(mant > 0.5, ex, ex - 1) + 127
    byte = np.clip(np.where(amax > 0, byte, 1), 1, 254)
    scaled = (w * np.exp2(127.0 - byte)[:, None, :]).reshape(k, n).astype(np.float32)
    by_word = np.ascontiguousarray(scaled.reshape(k // 512, 128, 4, n).transpose(0, 1, 3, 2))
    if fmt == "e4m3":
        words = by_word.astype(ml_dtypes.float8_e4m3fn).view(np.uint8)
    else:
        c = by_word.astype(ml_dtypes.float4_e2m1fn).view(np.uint8) & 0xF
        words = (c[..., 0::2] | (c[..., 1::2] << 4)).reshape(k // 512, 128, 2 * n)
    return np.ascontiguousarray(words), np.ascontiguousarray(byte.astype(np.uint8).reshape(k // 512, 16, n))


def unpack_weight(words, scales, fmt):
    g, _, n = scales.shape
    words = np.ascontiguousarray(words).reshape(g, 128, n, -1)
    if fmt == "e4m3":
        vals = words.view(ml_dtypes.float8_e4m3fn).astype(np.float64)
    else:
        nib = np.empty((g, 128, n, 4), np.uint8)
        nib[..., 0::2] = words & 0xF
        nib[..., 1::2] = words >> 4
        vals = E2M1[nib]
    vals = vals * np.repeat(np.exp2(scales.astype(np.float64) - 127.0), 8, axis=1)[..., None]
    return vals.transpose(0, 1, 3, 2).reshape(g * 512, n)


def gelu(v):
    return 0.5 * v * (1.0 + np.tanh(np.sqrt(2.0 / np.pi) * (v + 0.044715 * v**3)))


K, T, S, S2, H = 1024, 2048, 512, 1024, 512

def setup_inputs():
    n = np.random.standard_normal
    s = mx_kscale(K)[:, None]
    u = mx_kscale(H)[:, None]
    d = {}
    d["tab_words"], d["tab_scales"] = pack_weight(n((K, T)) * s, "e4m3")
    d["offs"] = striped(np.random.permutation(T)[:S])
    d["offs2"] = striped(np.random.permutation(T)[:S2])
    w1 = n((K, K)) / K**0.5 / K**0.5
    d["w1"] = (w1 / s / s.T).astype(np.float32)
    w2 = n((K, H)) / K**0.5
    d["w2"] = (w2 / s * u.T).astype(np.float32)
    d["w4_words"], d["w4_scales"] = pack_weight(1.4 * n((H, S)) / H**0.5 / u, "e2m1")
    d["kg"] = np.exp(0.3 * n(S2)).astype(np.float32)
    return d

def reference(tab_words, tab_scales, offs, offs2, w1, w2, w4_words, w4_scales, kg):
    TW = unpack_weight(tab_words, tab_scales, "e4m3")
    v = TW[:, unstriped(offs)]
    v2 = TW[:, unstriped(offs2)]
    h = np.abs(mxq(f64(w1), 0, "e4m3").T @ v)
    e = v2.T @ mxq(h, 0, "e4m3")
    b = np.abs(mxq(f64(w2), 0, "e4m3").T @ v2)
    w4 = unpack_weight(w4_words, w4_scales, "e2m1")
    f = mxq(b, 0, "e4m3").T @ w4
    return f64(kg)[:, None] * e * np.exp(-np.abs(f))

@@ -1,0 +1,225 @@
+from contextlib import ExitStack
+
+import concourse.mybir as mybir
+
+K, T, S, S2, H = 1024, 2048, 512, 1024, 512
+FLOPS = 2 * (K * K * S + K * S2 * S + K * H * S2 + H * S2 * S)
+
+F32 = mybir.dt.float32
+BF16 = mybir.dt.bfloat16
+I32 = mybir.dt.int32
+U32 = mybir.dt.uint32
+U16 = mybir.dt.uint16
+U8 = mybir.dt.uint8
+E4M3 = mybir.dt.float8_e4m3fn_x4
+E2M1 = mybir.dt.float4_e2m1fn_x4
+ACT = mybir.ActivationFunctionType
+ALU = mybir.AluOpType
+
+P = 128
+PACK = 4
+KP = P * PACK
+PASSES = K // KP
+M_TILES = S2 // P
+J_TILES = S // P
+PER_COL = 16
+EARLY = 1
+
+
+def tile_list_sash_kimono_harmony_kernel(
+    tc, tab_words, tab_scales, offs, offs2, w1, w2, w4_words, w4_scales, kg, out
+):
+    nc = tc.nc
+    with ExitStack() as ctx:
+        lists = ctx.enter_context(tc.tile_pool(name="lists", bufs=1))
+        sb = ctx.enter_context(tc.tile_pool(name="sb", bufs=1))
+        psum = ctx.enter_context(tc.psum_pool(name="psum", bufs=1))
+
+        def tile(name, shape, dtype, tag=None):
+            return sb.tile(shape, dtype, name=name, tag=tag or name, align_bytes=64)
+
+        def bank(b, name, shape):
+            return psum.tile(shape, F32, name=name, tag="bank%d" % b)
+
+        tab_plane = tile("tab_plane", [P, T], U8)
+        nc.vector.memset(tab_plane[:].bitcast(I32), 0)
+        w4_plane = tile("w4_plane", [P, S], U8)
+        nc.vector.memset(w4_plane[:].bitcast(I32), 0)
+        warm = tile("warm", [P, 2], F32)
+        nc.vector.memset(warm[:, 0:1], 0.0)
+        nc.scalar.activation(warm[:, 1:2], warm[:, 0:1], ACT.Exp)
+
+        idx2 = lists.tile([P, S2 // PER_COL], U16, name="idx2")
+        idx = lists.tile([P, S // PER_COL], U16, name="idx")
+        tab = [tile("tab%d" % a, [P, T], I32) for a in range(PASSES)]
+        w2_raw = [tile("w2_raw%d" % a, [P, PACK, KP], F32) for a in range(PASSES)]
+        w1_raw = {}
+
+        def load_tab(a):
+            nc.sync.dma_start(tab[a][:], tab_words[a].rearrange("p t i -> p (t i)").bitcast(I32))
+
+        def load_w(dst, w, a, g):
+            rows = w[KP * a : KP * (a + 1), KP * g : KP * (g + 1)]
+            nc.sync.dma_start(dst[:], rows.rearrange("(p i) c -> p i c", i=PACK))
+
+        def load_w1(g, a):
+            w1_raw[g, a] = tile("w1_raw%d%d" % (g, a), [P, PACK, KP], F32)
+            load_w(w1_raw[g, a], w1, a, g)
+
+        nc.sync.dma_start(idx2[:], offs2)
+        load_tab(0)
+        for q in range(4):
+            nc.sync.dma_start(
+                tab_plane[32 * q : 32 * q + 4 * PASSES, :].bitcast(I32),
+                tab_scales[:, 4 * q : 4 * q + 4, :].bitcast(I32),
+            )
+        load_w(w2_raw[0], w2, 0, 0)
+        load_w(w2_raw[1], w2, 1, 0)
+        nc.sync.dma_start(idx[:], offs)
+        load_tab(1)
+        load_w1(0, 0)
+        w4 = tile("w4", [P, 2 * S], U8)
+        nc.sync.dma_start(w4[:].bitcast(I32), w4_words[0].bitcast(I32))
+        for q in range(4):
+            nc.sync.dma_start(
+                w4_plane[32 * q : 32 * q + 4, :].bitcast(I32), w4_scales[0, 4 * q : 4 * q + 4, :].bitcast(I32)
+            )
+        load_w1(0, 1)
+        load_w1(1, 0)
+        load_w1(1, 1)
+        kg_col = tile("kg_col", [P, M_TILES], F32)
+        with nc.allow_non_contiguous_dma(reason="one gain to a partition"):
+            nc.sync.dma_start(kg_col[:], kg.rearrange("(t p) -> p t", p=P))
+
+        def gather(dst, window, offsets, lo, hi):
+            nc.vector.tensor_copy(dst[:, lo:hi], window.indirect(offsets[:, lo // PER_COL : hi // PER_COL]))
+
+        def cast(name, raw, half, on_scalar):
+            grouped = tile(name, [P, 2, P, PACK], BF16)
+            dst = grouped[:].rearrange("p t m i -> p m i t")
+            src = raw[:].rearrange("p i (m t) -> p m i t", t=PACK)[:, :, :, 2 * half : 2 * half + 2]
+            if on_scalar:
+                nc.scalar.copy(dst, src)
+            else:
+                nc.vector.tensor_copy(dst, src)
+            return grouped[:].rearrange("p t m i -> p (t m i)")
+
+        def quantise(codes, plane, values):
+            nc.vector.quantize_mx(out=codes.bitcast(E4M3), scales=plane, in_=values)
+
+        def quantise_new(name, values):
+            width = values.shape[1] // PACK
+            codes = tile(name + "_codes", [P, width], U32)
+            plane = tile(name + "_plane", [P, width], U8)
+            quantise(codes[:], plane[:], values)
+            return codes, plane
+
+        def weight_pass(acc, wq, words, plane, a, cols):
+            for t in range(PACK):
+                codes, wplane = wq[t // 2]
+                m = slice(P * (t % 2), P * (t % 2 + 1))
+                nc.tensor.matmul_mx(
+                    out=acc[:, t, :],
+                    lhsT=codes[:, m].bitcast(E4M3),
+                    lhsT_scale=wplane[:, m],
+                    rhs=words[:, cols].bitcast(E4M3),
+                    rhs_scale=plane[4 * a : P, cols],
+                    start=(a == 0 and t == 0),
+                    stop=(a == PASSES - 1 and t == PACK - 1),
+                )
+
+        def abs_out(grouped, c, acc):
+            nc.scalar.activation(grouped[:, P * c : P * (c + 1), :], acc[:].rearrange("p t n -> p n t"), ACT.Abs)
+
+        v2 = [tile("v2_%d" % a, [P, S2], U32) for a in range(PASSES)]
+        v2_plane = tile("v2_plane", [P, S2], U8)
+        v = [tile("v_%d" % a, [P, S], U32) for a in range(PASSES)]
+        v_plane = tile("v_plane", [P, S], U8)
+
+        gather(v2[0], tab[0][:].bitcast(U32), idx2, 0, S2)
+        gather(v2_plane, tab_plane[:], idx2, 0, S2)
+        w2_vals = {}
+        w2_vals[0, 0] = cast("w2g00", w2_raw[0], 0, True)
+        w2_vals[0, 1] = cast("w2g01", w2_raw[0], 1, True)
+        w2_vals[1, 0] = cast("w2g10", w2_raw[1], 0, True)
+        w2_vals[1, 1] = cast("w2g11", w2_raw[1], 1, True)
+        w2q = [[None, None], [None, None]]
+        for a, half in ((0, 0), (0, 1), (1, 0), (1, 1)):
+            w2q[a][half] = quantise_new("w2q%d%d" % (a, half), w2_vals[a, half])
+        b_vals = [tile("b_vals%d" % u, [P, KP, PACK], BF16) for u in range(2)]
+        bq = []
+        for u in range(4):
+            gather(v2[1], tab[1][:].bitcast(U32), idx2, 256 * u, 256 * (u + 1))
+            for c in (2 * u, 2 * u + 1):
+                b_acc = bank(c % 4, "b_acc%d" % c, [P, PACK, P])
+                for a in range(PASSES):
+                    weight_pass(b_acc, w2q[a], v2[a], v2_plane, a, slice(P * c, P * (c + 1)))
+                abs_out(b_vals[c // 4], c % 4, b_acc)
+        for u in range(2):
+            bq.append(quantise_new("bq%d" % u, b_vals[u][:].rearrange("p n t -> p (n t)")))
+
+        f_abs = []
+        for i in range(M_TILES):
+            f_acc = bank((i + 4) % 8, "f_acc%d" % i, [P, S])
+            codes, plane = bq[i // 4]
+            m = slice(P * (i % 4), P * (i % 4 + 1))
+            nc.tensor.matmul_mx(
+                out=f_acc[:],
+                lhsT=codes[:, m].bitcast(E4M3),
+                lhsT_scale=plane[:, m],
+                rhs=w4[:].bitcast(E2M1),
+                rhs_scale=w4_plane[:],
+                start=True,
+                stop=True,
+            )
+            fa = tile("f_abs%d" % i, [P, S], F32)
+            nc.scalar.activation(fa[:], f_acc[:], ACT.Abs)
+            f_abs.append(fa)
+
+        gather(v[0], tab[0][:].bitcast(U32), idx, 0, S)
+        gather(v_plane, tab_plane[:], idx, 0, S)
+        gather(v[1], tab[1][:].bitcast(U32), idx, 0, S)
+        h_all = []
+        for g in range(PASSES):
+            h_acc = [bank(4 * (1 - g) + c, "h_acc%d%d" % (g, c), [P, PACK, P]) for c in range(J_TILES)]
+            h_vals = tile("h_vals%d" % g, [P, S, PACK], BF16)
+            for a in range(PASSES):
+                vals = [cast("w1g%d%d%d" % (g, a, half), w1_raw[g, a], half, False) for half in range(2)]
+                wq = [quantise_new("w1q%d%d%d" % (g, a, half), vals[half]) for half in range(2)]
+                for c in range(J_TILES):
+                    weight_pass(h_acc[c], wq, v[a], v_plane, a, slice(P * c, P * (c + 1)))
+                    if a == PASSES - 1:
+                        abs_out(h_vals, c, h_acc[c])
+            h_all.append(h_vals)
+        h_codes = [tile("h_codes%d" % g, [P, S], U32, ("w1g111", None)[g]) for g in range(PASSES)]
+        h_plane = [tile("h_plane%d" % g, [P, S], U8) for g in range(PASSES)]
+        for g in range(PASSES):
+            h_vals = h_all[g]
+            step = S if g == 0 else P
+            for lo in range(0, S, step):
+                quantise(
+                    h_codes[g][:, lo : lo + step],
+                    h_plane[g][:, lo : lo + step],
+                    h_vals[:, lo : lo + step, :].rearrange("p n t -> p (n t)"),
+                )
+
+        damp_early = tile("damp_early", [P, EARLY, S], F32)
+        damp_late = tile("damp_late", [P, M_TILES - EARLY, S], F32, "v_1")
+        for i in range(M_TILES):
+            m = slice(P * i, P * (i + 1))
+            damp = damp_early[:, i, :] if i < EARLY else damp_late[:, i - EARLY, :]
+            nc.scalar.activation(damp, f_abs[i][:], ACT.Exp, scale=-1.0)
+            e_acc = bank((i + 4) % 8, "e_acc%d" % i, [P, S])
+            for g in range(PASSES):
+                nc.tensor.matmul_mx(
+                    out=e_acc[:],
+                    lhsT=v2[g][:, m].bitcast(E4M3),
+                    lhsT_scale=v2_plane[4 * g : P, m],
+                    rhs=h_codes[g][:].bitcast(E4M3),
+                    rhs_scale=h_plane[g][:],
+                    start=(g == 0),
+                    stop=(g == PASSES - 1),
+                )
+            res = tile("res%d" % i, [P, S], F32)
+            nc.vector.scalar_tensor_tensor(res[:], e_acc[:], kg_col[:, i : i + 1], damp, ALU.mult, ALU.mult)
+            nc.sync.dma_start(out[m, :], res[:])

@@ -23,7 +23,7 @@ PASSES = K // KP
 M_TILES = S2 // P
 J_TILES = S // P
 PER_COL = 16
-EARLY = 1
+SPLIT = 3
 
 
 def tile_list_sash_kimono_harmony_kernel(
@@ -42,7 +42,7 @@ def tile_list_sash_kimono_harmony_kernel(
             return psum.tile(shape, F32, name=name, tag="bank%d" % b)
 
         tab_plane = tile("tab_plane", [P, T], U8)
-        nc.vector.memset(tab_plane[:].bitcast(I32), 0)
+        nc.gpsimd.memset(tab_plane[:].bitcast(I32), 0)
         w4_plane = tile("w4_plane", [P, S], U8)
         nc.vector.memset(w4_plane[:].bitcast(I32), 0)
         warm = tile("warm", [P, 2], F32)
@@ -69,7 +69,7 @@ def tile_list_sash_kimono_harmony_kernel(
         nc.sync.dma_start(idx2[:], offs2)
         load_tab(0)
         for q in range(4):
-            nc.sync.dma_start(
+            nc.gpsimd.dma_start(
                 tab_plane[32 * q : 32 * q + 4 * PASSES, :].bitcast(I32),
                 tab_scales[:, 4 * q : 4 * q + 4, :].bitcast(I32),
             )
@@ -134,7 +134,6 @@ def tile_list_sash_kimono_harmony_kernel(
         v2 = [tile("v2_%d" % a, [P, S2], U32) for a in range(PASSES)]
         v2_plane = tile("v2_plane", [P, S2], U8)
         v = [tile("v_%d" % a, [P, S], U32) for a in range(PASSES)]
-        v_plane = tile("v_plane", [P, S], U8)
 
         gather(v2[0], tab[0][:].bitcast(U32), idx2, 0, S2)
         gather(v2_plane, tab_plane[:], idx2, 0, S2)
@@ -146,7 +145,7 @@ def tile_list_sash_kimono_harmony_kernel(
         w2q = [[None, None], [None, None]]
         for a, half in ((0, 0), (0, 1), (1, 0), (1, 1)):
             w2q[a][half] = quantise_new("w2q%d%d" % (a, half), w2_vals[a, half])
-        b_vals = [tile("b_vals%d" % u, [P, KP, PACK], BF16) for u in range(2)]
+        b_vals = [tile("b_vals%d" % u, [P, 2 * P, PACK], BF16) for u in range(4)]
         bq = []
         for u in range(4):
             gather(v2[1], tab[1][:].bitcast(U32), idx2, 256 * u, 256 * (u + 1))
@@ -154,15 +153,15 @@ def tile_list_sash_kimono_harmony_kernel(
                 b_acc = bank(c % 4, "b_acc%d" % c, [P, PACK, P])
                 for a in range(PASSES):
                     weight_pass(b_acc, w2q[a], v2[a], v2_plane, a, slice(P * c, P * (c + 1)))
-                abs_out(b_vals[c // 4], c % 4, b_acc)
-        for u in range(2):
+                abs_out(b_vals[u], c % 2, b_acc)
+        for u in range(4):
             bq.append(quantise_new("bq%d" % u, b_vals[u][:].rearrange("p n t -> p (n t)")))
 
         f_abs = []
         for i in range(M_TILES):
             f_acc = bank((i + 4) % 8, "f_acc%d" % i, [P, S])
-            codes, plane = bq[i // 4]
-            m = slice(P * (i % 4), P * (i % 4 + 1))
+            codes, plane = bq[i // 2]
+            m = slice(P * (i % 2), P * (i % 2 + 1))
             nc.tensor.matmul_mx(
                 out=f_acc[:],
                 lhsT=codes[:, m].bitcast(E4M3),
@@ -177,8 +176,9 @@ def tile_list_sash_kimono_harmony_kernel(
             f_abs.append(fa)
 
         gather(v[0], tab[0][:].bitcast(U32), idx, 0, S)
-        gather(v_plane, tab_plane[:], idx, 0, S)
         gather(v[1], tab[1][:].bitcast(U32), idx, 0, S)
+        v_plane = tile("v_plane", [P, S], U8, "w2q10_codes")
+        gather(v_plane, tab_plane[:], idx, 0, S)
         h_all = []
         for g in range(PASSES):
             h_acc = [bank(4 * (1 - g) + c, "h_acc%d%d" % (g, c), [P, PACK, P]) for c in range(J_TILES)]
@@ -203,23 +203,36 @@ def tile_list_sash_kimono_harmony_kernel(
                     h_vals[:, lo : lo + step, :].rearrange("p n t -> p (n t)"),
                 )
 
-        damp_early = tile("damp_early", [P, EARLY, S], F32)
-        damp_late = tile("damp_late", [P, M_TILES - EARLY, S], F32, "v_1")
-        for i in range(M_TILES):
+        half = S // 2
+        damp_early = tile("damp_early", [P, SPLIT, half], F32)
+        damp_late = tile("damp_late", [P, M_TILES, S], F32, "v_1")
+        res = [tile("res%d" % i, [P, S], F32) for i in range(M_TILES)]
+
+        def finish(i, lo, hi, damp):
             m = slice(P * i, P * (i + 1))
-            damp = damp_early[:, i, :] if i < EARLY else damp_late[:, i - EARLY, :]
-            nc.scalar.activation(damp, f_abs[i][:], ACT.Exp, scale=-1.0)
-            e_acc = bank((i + 4) % 8, "e_acc%d" % i, [P, S])
+            nc.scalar.activation(damp, f_abs[i][:, lo:hi], ACT.Exp, scale=-1.0)
+            e_acc = bank((i + 4) % 8, "e_acc%d_%d" % (i, lo), [P, hi - lo])
             for g in range(PASSES):
                 nc.tensor.matmul_mx(
                     out=e_acc[:],
                     lhsT=v2[g][:, m].bitcast(E4M3),
                     lhsT_scale=v2_plane[4 * g : P, m],
-                    rhs=h_codes[g][:].bitcast(E4M3),
-                    rhs_scale=h_plane[g][:],
+                    rhs=h_codes[g][:, lo:hi].bitcast(E4M3),
+                    rhs_scale=h_plane[g][:, lo:hi],
                     start=(g == 0),
                     stop=(g == PASSES - 1),
                 )
-            res = tile("res%d" % i, [P, S], F32)
-            nc.vector.scalar_tensor_tensor(res[:], e_acc[:], kg_col[:, i : i + 1], damp, ALU.mult, ALU.mult)
-            nc.sync.dma_start(out[m, :], res[:])
+            step = half if i == M_TILES - 1 else hi - lo
+            for c in range(0, hi - lo, step):
+                cols = slice(lo + c, lo + c + step)
+                nc.vector.scalar_tensor_tensor(
+                    res[i][:, cols], e_acc[:, c : c + step], kg_col[:, i : i + 1], damp[:, c : c + step], ALU.mult, ALU.mult
+                )
+                nc.sync.dma_start(out[m, cols], res[i][:, cols])
+
+        for i in range(SPLIT):
+            finish(i, 0, half, damp_early[:, i, :])
+        for i in range(SPLIT):
+            finish(i, half, S, damp_late[:, i, half:S])
+        for i in range(SPLIT, M_TILES):
+            finish(i, 0, S, damp_late[:, i, :])

@@ -1,6 +1,7 @@
 from contextlib import ExitStack
 
 import concourse.mybir as mybir
+from concourse.masks import make_identity
 
 K, T, S, S2, H = 1024, 2048, 512, 1024, 512
 FLOPS = 2 * (K * K * S + K * S2 * S + K * H * S2 + H * S2 * S)
@@ -42,12 +43,16 @@ def tile_list_sash_kimono_harmony_kernel(
             return psum.tile(shape, F32, name=name, tag="bank%d" % b)
 
         tab_plane = tile("tab_plane", [P, T], U8)
-        nc.gpsimd.memset(tab_plane[:].bitcast(I32), 0)
+        nc.vector.memset(tab_plane[:].bitcast(I32), 0)
         w4_plane = tile("w4_plane", [P, S], U8)
         nc.vector.memset(w4_plane[:].bitcast(I32), 0)
         warm = tile("warm", [P, 2], F32)
         nc.vector.memset(warm[:, 0:1], 0.0)
         nc.scalar.activation(warm[:, 1:2], warm[:, 0:1], ACT.Exp)
+        kg_rows = tile("kg_rows", [P, P], F32)
+        nc.vector.memset(kg_rows[:], 0.0)
+        ident = tile("ident", [P, P], F32)
+        make_identity(nc, ident[:])
 
         idx2 = lists.tile([P, S2 // PER_COL], U16, name="idx2")
         idx = lists.tile([P, S // PER_COL], U16, name="idx")
@@ -67,17 +72,18 @@ def tile_list_sash_kimono_harmony_kernel(
             load_w(w1_raw[g, a], w1, a, g)
 
         nc.sync.dma_start(idx2[:], offs2)
-        load_tab(0)
+        nc.sync.dma_start(idx[:], offs)
         for q in range(4):
-            nc.gpsimd.dma_start(
+            nc.sync.dma_start(
                 tab_plane[32 * q : 32 * q + 4 * PASSES, :].bitcast(I32),
                 tab_scales[:, 4 * q : 4 * q + 4, :].bitcast(I32),
             )
+        load_tab(0)
         load_w(w2_raw[0], w2, 0, 0)
         load_w(w2_raw[1], w2, 1, 0)
-        nc.sync.dma_start(idx[:], offs)
         load_tab(1)
         load_w1(0, 0)
+        nc.sync.dma_start(kg_rows[0:M_TILES, :], kg.rearrange("(t p) -> t p", p=P))
         w4 = tile("w4", [P, 2 * S], U8)
         nc.sync.dma_start(w4[:].bitcast(I32), w4_words[0].bitcast(I32))
         for q in range(4):
@@ -87,9 +93,6 @@ def tile_list_sash_kimono_harmony_kernel(
         load_w1(0, 1)
         load_w1(1, 0)
         load_w1(1, 1)
-        kg_col = tile("kg_col", [P, M_TILES], F32)
-        with nc.allow_non_contiguous_dma(reason="one gain to a partition"):
-            nc.sync.dma_start(kg_col[:], kg.rearrange("(t p) -> p t", p=P))
 
         def gather(dst, window, offsets, lo, hi):
             nc.vector.tensor_copy(dst[:, lo:hi], window.indirect(offsets[:, lo // PER_COL : hi // PER_COL]))
@@ -141,7 +144,7 @@ def tile_list_sash_kimono_harmony_kernel(
         w2_vals[0, 0] = cast("w2g00", w2_raw[0], 0, True)
         w2_vals[0, 1] = cast("w2g01", w2_raw[0], 1, True)
         w2_vals[1, 0] = cast("w2g10", w2_raw[1], 0, True)
-        w2_vals[1, 1] = cast("w2g11", w2_raw[1], 1, True)
+        w2_vals[1, 1] = cast("w2g11", w2_raw[1], 1, False)
         w2q = [[None, None], [None, None]]
         for a, half in ((0, 0), (0, 1), (1, 0), (1, 1)):
             w2q[a][half] = quantise_new("w2q%d%d" % (a, half), w2_vals[a, half])
@@ -156,6 +159,11 @@ def tile_list_sash_kimono_harmony_kernel(
                 abs_out(b_vals[u], c % 2, b_acc)
         for u in range(4):
             bq.append(quantise_new("bq%d" % u, b_vals[u][:].rearrange("p n t -> p (n t)")))
+
+        kg_ps = bank(7, "kg_ps", [P, P])
+        nc.tensor.transpose(kg_ps[:], kg_rows[:], ident[:])
+        kg_col = tile("kg_col", [P, M_TILES], F32)
+        nc.scalar.copy(kg_col[:], kg_ps[:, 0:M_TILES])
 
         f_abs = []
         for i in range(M_TILES):
@@ -177,7 +185,7 @@ def tile_list_sash_kimono_harmony_kernel(
 
         gather(v[0], tab[0][:].bitcast(U32), idx, 0, S)
         gather(v[1], tab[1][:].bitcast(U32), idx, 0, S)
-        v_plane = tile("v_plane", [P, S], U8, "w2q10_codes")
+        v_plane = tile("v_plane", [P, S], U8)
         gather(v_plane, tab_plane[:], idx, 0, S)
         h_all = []
         for g in range(PASSES):

@@ -21,9 +21,16 @@ P = 128
 PACK = 4
 KP = P * PACK
 PASSES = K // KP
+QUADS = 4
+QUAD = P // QUADS
+ROWS = 4
 M_TILES = S2 // P
 J_TILES = S // P
 PER_COL = 16
+HALVES = 2
+PAIR = 2 * P
+BANKS = 8
+RING = BANKS // 2
 SPLIT = 3
 
 
@@ -39,16 +46,13 @@ def tile_list_sash_kimono_harmony_kernel(
         def tile(name, shape, dtype, tag=None):
             return sb.tile(shape, dtype, name=name, tag=tag or name, align_bytes=64)
 
-        def bank(b, name, shape):
-            return psum.tile(shape, F32, name=name, tag="bank%d" % b)
+        def bank(number, name, shape):
+            return psum.tile(shape, F32, name=name, tag="bank%d" % number)
 
         tab_plane = tile("tab_plane", [P, T], U8)
         nc.vector.memset(tab_plane[:].bitcast(I32), 0)
         w4_plane = tile("w4_plane", [P, S], U8)
         nc.vector.memset(w4_plane[:].bitcast(I32), 0)
-        warm = tile("warm", [P, 2], F32)
-        nc.vector.memset(warm[:, 0:1], 0.0)
-        nc.scalar.activation(warm[:, 1:2], warm[:, 0:1], ACT.Exp)
         kg_rows = tile("kg_rows", [P, P], F32)
         nc.vector.memset(kg_rows[:], 0.0)
         ident = tile("ident", [P, P], F32)
@@ -73,10 +77,10 @@ def tile_list_sash_kimono_harmony_kernel(
 
         nc.sync.dma_start(idx2[:], offs2)
         nc.sync.dma_start(idx[:], offs)
-        for q in range(4):
+        for q in range(QUADS):
             nc.sync.dma_start(
-                tab_plane[32 * q : 32 * q + 4 * PASSES, :].bitcast(I32),
-                tab_scales[:, 4 * q : 4 * q + 4, :].bitcast(I32),
+                tab_plane[QUAD * q : QUAD * q + ROWS * PASSES, :].bitcast(I32),
+                tab_scales[:, ROWS * q : ROWS * (q + 1), :].bitcast(I32),
             )
         load_tab(0)
         load_w(w2_raw[0], w2, 0, 0)
@@ -86,9 +90,10 @@ def tile_list_sash_kimono_harmony_kernel(
         nc.sync.dma_start(kg_rows[0:M_TILES, :], kg.rearrange("(t p) -> t p", p=P))
         w4 = tile("w4", [P, 2 * S], U8)
         nc.sync.dma_start(w4[:].bitcast(I32), w4_words[0].bitcast(I32))
-        for q in range(4):
+        for q in range(QUADS):
             nc.sync.dma_start(
-                w4_plane[32 * q : 32 * q + 4, :].bitcast(I32), w4_scales[0, 4 * q : 4 * q + 4, :].bitcast(I32)
+                w4_plane[QUAD * q : QUAD * q + ROWS, :].bitcast(I32),
+                w4_scales[0, ROWS * q : ROWS * (q + 1), :].bitcast(I32),
             )
         load_w1(0, 1)
         load_w1(1, 0)
@@ -97,15 +102,12 @@ def tile_list_sash_kimono_harmony_kernel(
         def gather(dst, window, offsets, lo, hi):
             nc.vector.tensor_copy(dst[:, lo:hi], window.indirect(offsets[:, lo // PER_COL : hi // PER_COL]))
 
-        def cast(name, raw, half, on_scalar):
-            grouped = tile(name, [P, 2, P, PACK], BF16)
-            dst = grouped[:].rearrange("p t m i -> p m i t")
-            src = raw[:].rearrange("p i (m t) -> p m i t", t=PACK)[:, :, :, 2 * half : 2 * half + 2]
-            if on_scalar:
-                nc.scalar.copy(dst, src)
-            else:
-                nc.vector.tensor_copy(dst, src)
-            return grouped[:].rearrange("p t m i -> p (t m i)")
+        def round_weight(name, raw, half, copy):
+            rounded = tile(name, [P, HALVES, P, PACK], BF16)
+            dst = rounded[:].rearrange("p t m i -> p m i t")
+            src = raw[:].rearrange("p i (m t) -> p m i t", t=PACK)[:, :, :, HALVES * half : HALVES * (half + 1)]
+            copy(dst, src)
+            return rounded[:].rearrange("p t m i -> p (t m i)")
 
         def quantise(codes, plane, values):
             nc.vector.quantize_mx(out=codes.bitcast(E4M3), scales=plane, in_=values)
@@ -117,22 +119,22 @@ def tile_list_sash_kimono_harmony_kernel(
             quantise(codes[:], plane[:], values)
             return codes, plane
 
-        def weight_pass(acc, wq, words, plane, a, cols):
+        def weight_pass(acc, weight, words, plane, a, cols):
             for t in range(PACK):
-                codes, wplane = wq[t // 2]
-                m = slice(P * (t % 2), P * (t % 2 + 1))
+                w_codes, w_plane = weight[t // HALVES]
+                m = slice(P * (t % HALVES), P * (t % HALVES + 1))
                 nc.tensor.matmul_mx(
                     out=acc[:, t, :],
-                    lhsT=codes[:, m].bitcast(E4M3),
-                    lhsT_scale=wplane[:, m],
+                    lhsT=w_codes[:, m].bitcast(E4M3),
+                    lhsT_scale=w_plane[:, m],
                     rhs=words[:, cols].bitcast(E4M3),
-                    rhs_scale=plane[4 * a : P, cols],
+                    rhs_scale=plane[ROWS * a : P, cols],
                     start=(a == 0 and t == 0),
                     stop=(a == PASSES - 1 and t == PACK - 1),
                 )
 
-        def abs_out(grouped, c, acc):
-            nc.scalar.activation(grouped[:, P * c : P * (c + 1), :], acc[:].rearrange("p t n -> p n t"), ACT.Abs)
+        def abs_out(values, c, acc):
+            nc.scalar.activation(values[:, P * c : P * (c + 1), :], acc[:].rearrange("p t n -> p n t"), ACT.Abs)
 
         v2 = [tile("v2_%d" % a, [P, S2], U32) for a in range(PASSES)]
         v2_plane = tile("v2_plane", [P, S2], U8)
@@ -141,106 +143,110 @@ def tile_list_sash_kimono_harmony_kernel(
         gather(v2[0], tab[0][:].bitcast(U32), idx2, 0, S2)
         gather(v2_plane, tab_plane[:], idx2, 0, S2)
         w2_vals = {}
-        w2_vals[0, 0] = cast("w2g00", w2_raw[0], 0, True)
-        w2_vals[0, 1] = cast("w2g01", w2_raw[0], 1, True)
-        w2_vals[1, 0] = cast("w2g10", w2_raw[1], 0, True)
-        w2_vals[1, 1] = cast("w2g11", w2_raw[1], 1, False)
-        w2q = [[None, None], [None, None]]
-        for a, half in ((0, 0), (0, 1), (1, 0), (1, 1)):
-            w2q[a][half] = quantise_new("w2q%d%d" % (a, half), w2_vals[a, half])
-        b_vals = [tile("b_vals%d" % u, [P, 2 * P, PACK], BF16) for u in range(4)]
-        bq = []
-        for u in range(4):
-            gather(v2[1], tab[1][:].bitcast(U32), idx2, 256 * u, 256 * (u + 1))
-            for c in (2 * u, 2 * u + 1):
-                b_acc = bank(c % 4, "b_acc%d" % c, [P, PACK, P])
+        for a in range(PASSES):
+            for half in range(HALVES):
+                last = (a, half) == (PASSES - 1, HALVES - 1)
+                copy = nc.vector.tensor_copy if last else nc.scalar.copy
+                w2_vals[a, half] = round_weight("w2g%d%d" % (a, half), w2_raw[a], half, copy)
+        w2q = [
+            [quantise_new("w2q%d%d" % (a, half), w2_vals[a, half]) for half in range(HALVES)] for a in range(PASSES)
+        ]
+        b_vals = [tile("b_vals%d" % u, [P, PAIR, PACK], BF16) for u in range(S2 // PAIR)]
+        for u in range(S2 // PAIR):
+            gather(v2[1], tab[1][:].bitcast(U32), idx2, PAIR * u, PAIR * (u + 1))
+            for c in range(2):
+                i = 2 * u + c
+                b_acc = bank(i % RING, "b_acc%d" % i, [P, PACK, P])
                 for a in range(PASSES):
-                    weight_pass(b_acc, w2q[a], v2[a], v2_plane, a, slice(P * c, P * (c + 1)))
-                abs_out(b_vals[u], c % 2, b_acc)
-        for u in range(4):
-            bq.append(quantise_new("bq%d" % u, b_vals[u][:].rearrange("p n t -> p (n t)")))
+                    weight_pass(b_acc, w2q[a], v2[a], v2_plane, a, slice(P * i, P * (i + 1)))
+                abs_out(b_vals[u], c, b_acc)
+        bq = [quantise_new("bq%d" % u, b_vals[u][:].rearrange("p n t -> p (n t)")) for u in range(S2 // PAIR)]
 
-        kg_ps = bank(7, "kg_ps", [P, P])
+        kg_ps = bank(BANKS - 1, "kg_ps", [P, P])
         nc.tensor.transpose(kg_ps[:], kg_rows[:], ident[:])
         kg_col = tile("kg_col", [P, M_TILES], F32)
         nc.scalar.copy(kg_col[:], kg_ps[:, 0:M_TILES])
 
         f_abs = []
         for i in range(M_TILES):
-            f_acc = bank((i + 4) % 8, "f_acc%d" % i, [P, S])
-            codes, plane = bq[i // 2]
+            f_acc = bank((i + RING) % BANKS, "f_acc%d" % i, [P, S])
+            b_codes, b_plane = bq[i // 2]
             m = slice(P * (i % 2), P * (i % 2 + 1))
             nc.tensor.matmul_mx(
                 out=f_acc[:],
-                lhsT=codes[:, m].bitcast(E4M3),
-                lhsT_scale=plane[:, m],
+                lhsT=b_codes[:, m].bitcast(E4M3),
+                lhsT_scale=b_plane[:, m],
                 rhs=w4[:].bitcast(E2M1),
                 rhs_scale=w4_plane[:],
                 start=True,
                 stop=True,
             )
-            fa = tile("f_abs%d" % i, [P, S], F32)
-            nc.scalar.activation(fa[:], f_acc[:], ACT.Abs)
-            f_abs.append(fa)
+            f_abs.append(tile("f_abs%d" % i, [P, S], F32))
+            nc.scalar.activation(f_abs[i][:], f_acc[:], ACT.Abs)
 
         gather(v[0], tab[0][:].bitcast(U32), idx, 0, S)
         gather(v[1], tab[1][:].bitcast(U32), idx, 0, S)
         v_plane = tile("v_plane", [P, S], U8)
         gather(v_plane, tab_plane[:], idx, 0, S)
-        h_all = []
+        h_vals = []
         for g in range(PASSES):
-            h_acc = [bank(4 * (1 - g) + c, "h_acc%d%d" % (g, c), [P, PACK, P]) for c in range(J_TILES)]
-            h_vals = tile("h_vals%d" % g, [P, S, PACK], BF16)
+            h_acc = [bank(RING * (1 - g) + c, "h_acc%d%d" % (g, c), [P, PACK, P]) for c in range(J_TILES)]
+            h_vals.append(tile("h_vals%d" % g, [P, S, PACK], BF16))
             for a in range(PASSES):
-                vals = [cast("w1g%d%d%d" % (g, a, half), w1_raw[g, a], half, False) for half in range(2)]
-                wq = [quantise_new("w1q%d%d%d" % (g, a, half), vals[half]) for half in range(2)]
+                w1_vals = [
+                    round_weight("w1g%d%d%d" % (g, a, half), w1_raw[g, a], half, nc.vector.tensor_copy)
+                    for half in range(HALVES)
+                ]
+                w1q = [quantise_new("w1q%d%d%d" % (g, a, half), w1_vals[half]) for half in range(HALVES)]
                 for c in range(J_TILES):
-                    weight_pass(h_acc[c], wq, v[a], v_plane, a, slice(P * c, P * (c + 1)))
+                    weight_pass(h_acc[c], w1q, v[a], v_plane, a, slice(P * c, P * (c + 1)))
                     if a == PASSES - 1:
-                        abs_out(h_vals, c, h_acc[c])
-            h_all.append(h_vals)
-        h_codes = [tile("h_codes%d" % g, [P, S], U32, ("w1g111", None)[g]) for g in range(PASSES)]
+                        abs_out(h_vals[g], c, h_acc[c])
+        h_codes = [tile("h_codes0", [P, S], U32, "w1g111"), tile("h_codes1", [P, S], U32)]
         h_plane = [tile("h_plane%d" % g, [P, S], U8) for g in range(PASSES)]
-        for g in range(PASSES):
-            h_vals = h_all[g]
-            step = S if g == 0 else P
-            for lo in range(0, S, step):
+        for g, width in enumerate((S, P)):
+            for lo in range(0, S, width):
                 quantise(
-                    h_codes[g][:, lo : lo + step],
-                    h_plane[g][:, lo : lo + step],
-                    h_vals[:, lo : lo + step, :].rearrange("p n t -> p (n t)"),
+                    h_codes[g][:, lo : lo + width],
+                    h_plane[g][:, lo : lo + width],
+                    h_vals[g][:, lo : lo + width, :].rearrange("p n t -> p (n t)"),
                 )
 
-        half = S // 2
-        damp_early = tile("damp_early", [P, SPLIT, half], F32)
+        mid = S // 2
+        damp_early = tile("damp_early", [P, SPLIT, mid], F32)
         damp_late = tile("damp_late", [P, M_TILES, S], F32, "v_1")
         res = [tile("res%d" % i, [P, S], F32) for i in range(M_TILES)]
 
         def finish(i, lo, hi, damp):
             m = slice(P * i, P * (i + 1))
             nc.scalar.activation(damp, f_abs[i][:, lo:hi], ACT.Exp, scale=-1.0)
-            e_acc = bank((i + 4) % 8, "e_acc%d_%d" % (i, lo), [P, hi - lo])
+            e_acc = bank((i + RING) % BANKS, "e_acc%d_%d" % (i, lo), [P, hi - lo])
             for g in range(PASSES):
                 nc.tensor.matmul_mx(
                     out=e_acc[:],
                     lhsT=v2[g][:, m].bitcast(E4M3),
-                    lhsT_scale=v2_plane[4 * g : P, m],
+                    lhsT_scale=v2_plane[ROWS * g : P, m],
                     rhs=h_codes[g][:, lo:hi].bitcast(E4M3),
                     rhs_scale=h_plane[g][:, lo:hi],
                     start=(g == 0),
                     stop=(g == PASSES - 1),
                 )
-            step = half if i == M_TILES - 1 else hi - lo
-            for c in range(0, hi - lo, step):
-                cols = slice(lo + c, lo + c + step)
+            piece = mid if i == M_TILES - 1 else hi - lo
+            for at in range(0, hi - lo, piece):
+                cols = slice(lo + at, lo + at + piece)
                 nc.vector.scalar_tensor_tensor(
-                    res[i][:, cols], e_acc[:, c : c + step], kg_col[:, i : i + 1], damp[:, c : c + step], ALU.mult, ALU.mult
+                    res[i][:, cols],
+                    e_acc[:, at : at + piece],
+                    kg_col[:, i : i + 1],
+                    damp[:, at : at + piece],
+                    ALU.mult,
+                    ALU.mult,
                 )
                 nc.sync.dma_start(out[m, cols], res[i][:, cols])
 
         for i in range(SPLIT):
-            finish(i, 0, half, damp_early[:, i, :])
+            finish(i, 0, mid, damp_early[:, i, :])
         for i in range(SPLIT):
-            finish(i, half, S, damp_late[:, i, half:S])
+            finish(i, mid, S, damp_late[:, i, mid:S])
         for i in range(SPLIT, M_TILES):
             finish(i, 0, S, damp_late[:, i, :])

from contextlib import ExitStack

import concourse.mybir as mybir
from concourse.masks import make_identity

K, T, S, S2, H = 1024, 2048, 512, 1024, 512
FLOPS = 2 * (K * K * S + K * S2 * S + K * H * S2 + H * S2 * S)

F32 = mybir.dt.float32
BF16 = mybir.dt.bfloat16
I32 = mybir.dt.int32
U32 = mybir.dt.uint32
U16 = mybir.dt.uint16
U8 = mybir.dt.uint8
E4M3 = mybir.dt.float8_e4m3fn_x4
E2M1 = mybir.dt.float4_e2m1fn_x4
ACT = mybir.ActivationFunctionType
ALU = mybir.AluOpType

P = 128
PACK = 4
KP = P * PACK
PASSES = K // KP
QUADS = 4
QUAD = P // QUADS
ROWS = 4
M_TILES = S2 // P
J_TILES = S // P
PER_COL = 16
HALVES = 2
PAIR = 2 * P
BANKS = 8
RING = BANKS // 2
SPLIT = 3


def tile_list_sash_kimono_harmony_kernel(
    tc, tab_words, tab_scales, offs, offs2, w1, w2, w4_words, w4_scales, kg, out
):
    nc = tc.nc
    with ExitStack() as ctx:
        lists = ctx.enter_context(tc.tile_pool(name="lists", bufs=1))
        sb = ctx.enter_context(tc.tile_pool(name="sb", bufs=1))
        psum = ctx.enter_context(tc.psum_pool(name="psum", bufs=1))

        def tile(name, shape, dtype, tag=None):
            return sb.tile(shape, dtype, name=name, tag=tag or name, align_bytes=64)

        def bank(number, name, shape):
            return psum.tile(shape, F32, name=name, tag="bank%d" % number)

        tab_plane = tile("tab_plane", [P, T], U8)
        nc.vector.memset(tab_plane[:].bitcast(I32), 0)
        w4_plane = tile("w4_plane", [P, S], U8)
        nc.vector.memset(w4_plane[:].bitcast(I32), 0)
        kg_rows = tile("kg_rows", [P, P], F32)
        nc.vector.memset(kg_rows[:], 0.0)
        ident = tile("ident", [P, P], F32)
        make_identity(nc, ident[:])

        idx2 = lists.tile([P, S2 // PER_COL], U16, name="idx2")
        idx = lists.tile([P, S // PER_COL], U16, name="idx")
        tab = [tile("tab%d" % a, [P, T], I32) for a in range(PASSES)]
        w2_raw = [tile("w2_raw%d" % a, [P, PACK, KP], F32) for a in range(PASSES)]
        w1_raw = {}

        def load_tab(a):
            nc.sync.dma_start(tab[a][:], tab_words[a].rearrange("p t i -> p (t i)").bitcast(I32))

        def load_w(dst, w, a, g):
            rows = w[KP * a : KP * (a + 1), KP * g : KP * (g + 1)]
            nc.sync.dma_start(dst[:], rows.rearrange("(p i) c -> p i c", i=PACK))

        def load_w1(g, a):
            w1_raw[g, a] = tile("w1_raw%d%d" % (g, a), [P, PACK, KP], F32)
            load_w(w1_raw[g, a], w1, a, g)

        nc.sync.dma_start(idx2[:], offs2)
        nc.sync.dma_start(idx[:], offs)
        for q in range(QUADS):
            nc.sync.dma_start(
                tab_plane[QUAD * q : QUAD * q + ROWS * PASSES, :].bitcast(I32),
                tab_scales[:, ROWS * q : ROWS * (q + 1), :].bitcast(I32),
            )
        load_tab(0)
        load_w(w2_raw[0], w2, 0, 0)
        load_w(w2_raw[1], w2, 1, 0)
        load_tab(1)
        load_w1(0, 0)
        nc.sync.dma_start(kg_rows[0:M_TILES, :], kg.rearrange("(t p) -> t p", p=P))
        w4 = tile("w4", [P, 2 * S], U8)
        nc.sync.dma_start(w4[:].bitcast(I32), w4_words[0].bitcast(I32))
        for q in range(QUADS):
            nc.sync.dma_start(
                w4_plane[QUAD * q : QUAD * q + ROWS, :].bitcast(I32),
                w4_scales[0, ROWS * q : ROWS * (q + 1), :].bitcast(I32),
            )
        load_w1(0, 1)
        load_w1(1, 0)
        load_w1(1, 1)

        def gather(dst, window, offsets, lo, hi):
            nc.vector.tensor_copy(dst[:, lo:hi], window.indirect(offsets[:, lo // PER_COL : hi // PER_COL]))

        def round_weight(name, raw, half, copy):
            rounded = tile(name, [P, HALVES, P, PACK], BF16)
            dst = rounded[:].rearrange("p t m i -> p m i t")
            src = raw[:].rearrange("p i (m t) -> p m i t", t=PACK)[:, :, :, HALVES * half : HALVES * (half + 1)]
            copy(dst, src)
            return rounded[:].rearrange("p t m i -> p (t m i)")

        def quantise(codes, plane, values):
            nc.vector.quantize_mx(out=codes.bitcast(E4M3), scales=plane, in_=values)

        def quantise_new(name, values):
            width = values.shape[1] // PACK
            codes = tile(name + "_codes", [P, width], U32)
            plane = tile(name + "_plane", [P, width], U8)
            quantise(codes[:], plane[:], values)
            return codes, plane

        def weight_pass(acc, weight, words, plane, a, cols):
            for t in range(PACK):
                w_codes, w_plane = weight[t // HALVES]
                m = slice(P * (t % HALVES), P * (t % HALVES + 1))
                nc.tensor.matmul_mx(
                    out=acc[:, t, :],
                    lhsT=w_codes[:, m].bitcast(E4M3),
                    lhsT_scale=w_plane[:, m],
                    rhs=words[:, cols].bitcast(E4M3),
                    rhs_scale=plane[ROWS * a : P, cols],
                    start=(a == 0 and t == 0),
                    stop=(a == PASSES - 1 and t == PACK - 1),
                )

        def abs_out(values, c, acc):
            nc.scalar.activation(values[:, P * c : P * (c + 1), :], acc[:].rearrange("p t n -> p n t"), ACT.Abs)

        v2 = [tile("v2_%d" % a, [P, S2], U32) for a in range(PASSES)]
        v2_plane = tile("v2_plane", [P, S2], U8)
        v = [tile("v_%d" % a, [P, S], U32) for a in range(PASSES)]

        gather(v2[0], tab[0][:].bitcast(U32), idx2, 0, S2)
        gather(v2_plane, tab_plane[:], idx2, 0, S2)
        w2_vals = {}
        for a in range(PASSES):
            for half in range(HALVES):
                last = (a, half) == (PASSES - 1, HALVES - 1)
                copy = nc.vector.tensor_copy if last else nc.scalar.copy
                w2_vals[a, half] = round_weight("w2g%d%d" % (a, half), w2_raw[a], half, copy)
        w2q = [
            [quantise_new("w2q%d%d" % (a, half), w2_vals[a, half]) for half in range(HALVES)] for a in range(PASSES)
        ]
        b_vals = [tile("b_vals%d" % u, [P, PAIR, PACK], BF16) for u in range(S2 // PAIR)]
        for u in range(S2 // PAIR):
            gather(v2[1], tab[1][:].bitcast(U32), idx2, PAIR * u, PAIR * (u + 1))
            for c in range(2):
                i = 2 * u + c
                b_acc = bank(i % RING, "b_acc%d" % i, [P, PACK, P])
                for a in range(PASSES):
                    weight_pass(b_acc, w2q[a], v2[a], v2_plane, a, slice(P * i, P * (i + 1)))
                abs_out(b_vals[u], c, b_acc)
        bq = [quantise_new("bq%d" % u, b_vals[u][:].rearrange("p n t -> p (n t)")) for u in range(S2 // PAIR)]

        kg_ps = bank(BANKS - 1, "kg_ps", [P, P])
        nc.tensor.transpose(kg_ps[:], kg_rows[:], ident[:])
        kg_col = tile("kg_col", [P, M_TILES], F32)
        nc.scalar.copy(kg_col[:], kg_ps[:, 0:M_TILES])

        f_abs = []
        for i in range(M_TILES):
            f_acc = bank((i + RING) % BANKS, "f_acc%d" % i, [P, S])
            b_codes, b_plane = bq[i // 2]
            m = slice(P * (i % 2), P * (i % 2 + 1))
            nc.tensor.matmul_mx(
                out=f_acc[:],
                lhsT=b_codes[:, m].bitcast(E4M3),
                lhsT_scale=b_plane[:, m],
                rhs=w4[:].bitcast(E2M1),
                rhs_scale=w4_plane[:],
                start=True,
                stop=True,
            )
            f_abs.append(tile("f_abs%d" % i, [P, S], F32))
            nc.scalar.activation(f_abs[i][:], f_acc[:], ACT.Abs)

        gather(v[0], tab[0][:].bitcast(U32), idx, 0, S)
        gather(v[1], tab[1][:].bitcast(U32), idx, 0, S)
        v_plane = tile("v_plane", [P, S], U8)
        gather(v_plane, tab_plane[:], idx, 0, S)
        h_vals = []
        for g in range(PASSES):
            h_acc = [bank(RING * (1 - g) + c, "h_acc%d%d" % (g, c), [P, PACK, P]) for c in range(J_TILES)]
            h_vals.append(tile("h_vals%d" % g, [P, S, PACK], BF16))
            for a in range(PASSES):
                w1_vals = [
                    round_weight("w1g%d%d%d" % (g, a, half), w1_raw[g, a], half, nc.vector.tensor_copy)
                    for half in range(HALVES)
                ]
                w1q = [quantise_new("w1q%d%d%d" % (g, a, half), w1_vals[half]) for half in range(HALVES)]
                for c in range(J_TILES):
                    weight_pass(h_acc[c], w1q, v[a], v_plane, a, slice(P * c, P * (c + 1)))
                    if a == PASSES - 1:
                        abs_out(h_vals[g], c, h_acc[c])
        h_codes = [tile("h_codes0", [P, S], U32, "w1g111"), tile("h_codes1", [P, S], U32)]
        h_plane = [tile("h_plane%d" % g, [P, S], U8) for g in range(PASSES)]
        for g, width in enumerate((S, P)):
            for lo in range(0, S, width):
                quantise(
                    h_codes[g][:, lo : lo + width],
                    h_plane[g][:, lo : lo + width],
                    h_vals[g][:, lo : lo + width, :].rearrange("p n t -> p (n t)"),
                )

        mid = S // 2
        damp_early = tile("damp_early", [P, SPLIT, mid], F32)
        damp_late = tile("damp_late", [P, M_TILES, S], F32, "v_1")
        res = [tile("res%d" % i, [P, S], F32) for i in range(M_TILES)]

        def finish(i, lo, hi, damp):
            m = slice(P * i, P * (i + 1))
            nc.scalar.activation(damp, f_abs[i][:, lo:hi], ACT.Exp, scale=-1.0)
            e_acc = bank((i + RING) % BANKS, "e_acc%d_%d" % (i, lo), [P, hi - lo])
            for g in range(PASSES):
                nc.tensor.matmul_mx(
                    out=e_acc[:],
                    lhsT=v2[g][:, m].bitcast(E4M3),
                    lhsT_scale=v2_plane[ROWS * g : P, m],
                    rhs=h_codes[g][:, lo:hi].bitcast(E4M3),
                    rhs_scale=h_plane[g][:, lo:hi],
                    start=(g == 0),
                    stop=(g == PASSES - 1),
                )
            piece = mid if i == M_TILES - 1 else hi - lo
            for at in range(0, hi - lo, piece):
                cols = slice(lo + at, lo + at + piece)
                nc.vector.scalar_tensor_tensor(
                    res[i][:, cols],
                    e_acc[:, at : at + piece],
                    kg_col[:, i : i + 1],
                    damp[:, at : at + piece],
                    ALU.mult,
                    ALU.mult,
                )
                nc.sync.dma_start(out[m, cols], res[i][:, cols])

        for i in range(SPLIT):
            finish(i, 0, mid, damp_early[:, i, :])
        for i in range(SPLIT):
            finish(i, mid, S, damp_late[:, i, mid:S])
        for i in range(SPLIT, M_TILES):
            finish(i, 0, S, damp_late[:, i, :])
